import numpy as np
import ml_dtypes

BF16 = ml_dtypes.bfloat16


def bf(x):
    return np.asarray(x, np.float32).astype(BF16)


def f32(x):
    return np.asarray(x, np.float32)


def f64(x):
    return np.asarray(x).astype(np.float64)


def striped(idx):
    return np.tile(idx.reshape(-1, 16).T, (8, 1))


S, K, M, N, D, V = 1024, 512, 128, 512, 2, 256


def setup_inputs():
    return {"table": bf(np.random.standard_normal((K, S))), "w": bf(np.random.standard_normal((D, K, M)) / np.sqrt(D * K)), "b": f32(0.5 * np.random.standard_normal((M, 1))), "offs": striped(np.random.permutation(S)[:N])}


def reference(table, w, b, offs):
    idx = offs[:16].T.reshape(-1)
    x = f64(table)[:, idx]
    y = sum(f64(w)[t].T @ x[:, t * V : (t + 1) * V] for t in range(D))
    return y + f64(b)

@@ -1,0 +1,57 @@
+import concourse.mybir as mybir
+
+BF16, F32, U16 = mybir.dt.bfloat16, mybir.dt.float32, mybir.dt.uint16
+
+P = 128
+NODES = 1024
+FEATURES = 512
+BLOCKS = FEATURES // P
+ENDS = 2
+EDGES = 256
+OUT_FEATURES = 128
+LIST_COLUMNS = EDGES // 16
+
+FLOPS = 2 * ENDS * FEATURES * OUT_FEATURES * EDGES
+
+
+def tile_gather_matmul_kernel(tc, table, w, b, offs, out):
+    nc = tc.nc
+    with (
+        tc.tile_pool(name="held", bufs=1) as held,
+        tc.psum_pool(name="psum", bufs=1) as psum,
+    ):
+        offsets = held.tile([P, ENDS * LIST_COLUMNS], U16, name="offsets")
+        nc.sync.dma_start(offsets[:], offs)
+
+        weights = held.tile([P, ENDS, BLOCKS, OUT_FEATURES], BF16, name="weights")
+        nc.scalar.dma_start(weights[:], w.rearrange("t (k p) m -> p t k m", p=P))
+
+        bias = held.tile([P, 1], F32, name="bias")
+        nc.gpsimd.dma_start(bias[:], b)
+
+        windows = []
+        for k in range(BLOCKS):
+            window = held.tile([P, NODES], BF16, name="window%d" % k)
+            queue = nc.sync if k % 2 == 0 else nc.scalar
+            queue.dma_start(window[:], table[k * P : (k + 1) * P, :])
+            windows.append(window)
+
+        edge_sums = psum.tile([P, EDGES], F32, name="edge_sums")
+        for k in range(BLOCKS):
+            for t in range(ENDS):
+                picked = windows[k][:].indirect(
+                    offsets[:, t * LIST_COLUMNS : (t + 1) * LIST_COLUMNS]
+                )
+                nc.tensor.matmul(
+                    edge_sums[:],
+                    weights[:, t, k, :],
+                    picked,
+                    start=(k == 0 and t == 0),
+                    stop=(k == BLOCKS - 1 and t == ENDS - 1),
+                )
+
+        result = held.tile([P, EDGES], F32, name="result")
+        nc.vector.tensor_scalar(
+            result[:], edge_sums[:], bias[:, 0:1], None, mybir.AluOpType.add
+        )
+        nc.sync.dma_start(out, result[:])

@@ -9,6 +9,8 @@ BLOCKS = FEATURES // P
 ENDS = 2
 EDGES = 256
 OUT_FEATURES = 128
+BANK_COLUMNS = 512
+WARMING_MATMULS = 4
 LIST_COLUMNS = EDGES // 16
 
 FLOPS = 2 * ENDS * FEATURES * OUT_FEATURES * EDGES
@@ -23,18 +25,27 @@ def tile_gather_matmul_kernel(tc, table, w, b, offs, out):
         offsets = held.tile([P, ENDS * LIST_COLUMNS], U16, name="offsets")
         nc.sync.dma_start(offsets[:], offs)
 
-        weights = held.tile([P, ENDS, BLOCKS, OUT_FEATURES], BF16, name="weights")
-        nc.scalar.dma_start(weights[:], w.rearrange("t (k p) m -> p t k m", p=P))
+        zeros = held.tile([P, BANK_COLUMNS], BF16, name="zeros")
+        nc.vector.memset(zeros[:], 0.0)
+        unread = psum.tile([P, BANK_COLUMNS], F32, name="unread")
+        for i in range(WARMING_MATMULS):
+            nc.tensor.matmul(unread[:], zeros[:, 0:P], zeros[:], start=True, stop=True)
+
+        w_ends = w.rearrange("t (p k) m -> t p k m", k=BLOCKS)
+        table_blocks = table.rearrange("(p k) s -> k p s", k=BLOCKS)
+        weights = [
+            held.tile([P, BLOCKS, OUT_FEATURES], BF16, name="weights%d" % t) for t in range(ENDS)
+        ]
+        windows = [held.tile([P, NODES], BF16, name="window%d" % k) for k in range(BLOCKS)]
+
+        nc.sync.dma_start(weights[0][:], w_ends[0])
+        nc.sync.dma_start(windows[0][:], table_blocks[0])
+        nc.sync.dma_start(weights[1][:], w_ends[1])
+        for k in range(1, BLOCKS):
+            nc.sync.dma_start(windows[k][:], table_blocks[k])
 
         bias = held.tile([P, 1], F32, name="bias")
-        nc.gpsimd.dma_start(bias[:], b)
-
-        windows = []
-        for k in range(BLOCKS):
-            window = held.tile([P, NODES], BF16, name="window%d" % k)
-            queue = nc.sync if k % 2 == 0 else nc.scalar
-            queue.dma_start(window[:], table[k * P : (k + 1) * P, :])
-            windows.append(window)
+        nc.scalar.dma_start(bias[:], b)
 
         edge_sums = psum.tile([P, EDGES], F32, name="edge_sums")
         for k in range(BLOCKS):
@@ -44,7 +55,7 @@ def tile_gather_matmul_kernel(tc, table, w, b, offs, out):
                 )
                 nc.tensor.matmul(
                     edge_sums[:],
-                    weights[:, t, k, :],
+                    weights[t][:, k, :],
                     picked,
                     start=(k == 0 and t == 0),
                     stop=(k == BLOCKS - 1 and t == ENDS - 1),

@@ -31,21 +31,18 @@ def tile_gather_matmul_kernel(tc, table, w, b, offs, out):
         for i in range(WARMING_MATMULS):
             nc.tensor.matmul(unread[:], zeros[:, 0:P], zeros[:], start=True, stop=True)
 
-        w_ends = w.rearrange("t (p k) m -> t p k m", k=BLOCKS)
-        table_blocks = table.rearrange("(p k) s -> k p s", k=BLOCKS)
-        weights = [
-            held.tile([P, BLOCKS, OUT_FEATURES], BF16, name="weights%d" % t) for t in range(ENDS)
-        ]
-        windows = [held.tile([P, NODES], BF16, name="window%d" % k) for k in range(BLOCKS)]
-
-        nc.sync.dma_start(weights[0][:], w_ends[0])
-        nc.sync.dma_start(windows[0][:], table_blocks[0])
-        nc.sync.dma_start(weights[1][:], w_ends[1])
-        for k in range(1, BLOCKS):
-            nc.sync.dma_start(windows[k][:], table_blocks[k])
-
         bias = held.tile([P, 1], F32, name="bias")
         nc.scalar.dma_start(bias[:], b)
+
+        w_blocks = w.rearrange("t (k p) m -> k p t m", p=P)
+        windows, weights = [], []
+        for k in range(BLOCKS):
+            weights_k = held.tile([P, ENDS, OUT_FEATURES], BF16, name="weights%d" % k)
+            nc.sync.dma_start(weights_k[:], w_blocks[k])
+            weights.append(weights_k)
+            window = held.tile([P, NODES], BF16, name="window%d" % k)
+            nc.sync.dma_start(window[:], table[k * P : (k + 1) * P, :])
+            windows.append(window)
 
         edge_sums = psum.tile([P, EDGES], F32, name="edge_sums")
         for k in range(BLOCKS):
@@ -55,7 +52,7 @@ def tile_gather_matmul_kernel(tc, table, w, b, offs, out):
                 )
                 nc.tensor.matmul(
                     edge_sums[:],
-                    weights[t][:, k, :],
+                    weights[k][:, t, :],
                     picked,
                     start=(k == 0 and t == 0),
                     stop=(k == BLOCKS - 1 and t == ENDS - 1),

@@ -9,8 +9,6 @@ BLOCKS = FEATURES // P
 ENDS = 2
 EDGES = 256
 OUT_FEATURES = 128
-BANK_COLUMNS = 512
-WARMING_MATMULS = 4
 LIST_COLUMNS = EDGES // 16
 
 FLOPS = 2 * ENDS * FEATURES * OUT_FEATURES * EDGES
@@ -25,24 +23,21 @@ def tile_gather_matmul_kernel(tc, table, w, b, offs, out):
         offsets = held.tile([P, ENDS * LIST_COLUMNS], U16, name="offsets")
         nc.sync.dma_start(offsets[:], offs)
 
-        zeros = held.tile([P, BANK_COLUMNS], BF16, name="zeros")
-        nc.vector.memset(zeros[:], 0.0)
-        unread = psum.tile([P, BANK_COLUMNS], F32, name="unread")
-        for i in range(WARMING_MATMULS):
-            nc.tensor.matmul(unread[:], zeros[:, 0:P], zeros[:], start=True, stop=True)
+        w_ends = w.rearrange("t (p k) m -> t p k m", k=BLOCKS)
+        table_blocks = table.rearrange("(p k) s -> k p s", k=BLOCKS)
+        weights = [
+            held.tile([P, BLOCKS, OUT_FEATURES], BF16, name="weights%d" % t) for t in range(ENDS)
+        ]
+        windows = [held.tile([P, NODES], BF16, name="window%d" % k) for k in range(BLOCKS)]
+
+        nc.sync.dma_start(weights[0][:], w_ends[0])
+        nc.sync.dma_start(windows[0][:], table_blocks[0])
+        nc.sync.dma_start(weights[1][:], w_ends[1])
+        for k in range(1, BLOCKS):
+            nc.sync.dma_start(windows[k][:], table_blocks[k])
 
         bias = held.tile([P, 1], F32, name="bias")
         nc.scalar.dma_start(bias[:], b)
-
-        w_blocks = w.rearrange("t (k p) m -> k p t m", p=P)
-        windows, weights = [], []
-        for k in range(BLOCKS):
-            weights_k = held.tile([P, ENDS, OUT_FEATURES], BF16, name="weights%d" % k)
-            nc.sync.dma_start(weights_k[:], w_blocks[k])
-            weights.append(weights_k)
-            window = held.tile([P, NODES], BF16, name="window%d" % k)
-            nc.sync.dma_start(window[:], table[k * P : (k + 1) * P, :])
-            windows.append(window)
 
         edge_sums = psum.tile([P, EDGES], F32, name="edge_sums")
         for k in range(BLOCKS):
@@ -52,7 +47,7 @@ def tile_gather_matmul_kernel(tc, table, w, b, offs, out):
                 )
                 nc.tensor.matmul(
                     edge_sums[:],
-                    weights[k][:, t, :],
+                    weights[t][:, k, :],
                     picked,
                     start=(k == 0 and t == 0),
                     stop=(k == BLOCKS - 1 and t == ENDS - 1),

@@ -23,21 +23,19 @@ def tile_gather_matmul_kernel(tc, table, w, b, offs, out):
         offsets = held.tile([P, ENDS * LIST_COLUMNS], U16, name="offsets")
         nc.sync.dma_start(offsets[:], offs)
 
-        w_ends = w.rearrange("t (p k) m -> t p k m", k=BLOCKS)
-        table_blocks = table.rearrange("(p k) s -> k p s", k=BLOCKS)
-        weights = [
-            held.tile([P, BLOCKS, OUT_FEATURES], BF16, name="weights%d" % t) for t in range(ENDS)
-        ]
-        windows = [held.tile([P, NODES], BF16, name="window%d" % k) for k in range(BLOCKS)]
-
-        nc.sync.dma_start(weights[0][:], w_ends[0])
-        nc.sync.dma_start(windows[0][:], table_blocks[0])
-        nc.sync.dma_start(weights[1][:], w_ends[1])
-        for k in range(1, BLOCKS):
-            nc.sync.dma_start(windows[k][:], table_blocks[k])
+        weights = held.tile([P, ENDS, BLOCKS, OUT_FEATURES], BF16, name="weights")
+        nc.scalar.dma_start(weights[:], w.rearrange("t (p k) m -> p t k m", k=BLOCKS))
 
         bias = held.tile([P, 1], F32, name="bias")
-        nc.scalar.dma_start(bias[:], b)
+        nc.gpsimd.dma_start(bias[:], b)
+
+        table_blocks = table.rearrange("(p k) s -> k p s", k=BLOCKS)
+        windows = []
+        for k in range(BLOCKS):
+            window = held.tile([P, NODES], BF16, name="window%d" % k)
+            queue = nc.sync if k % 2 == 0 else nc.scalar
+            queue.dma_start(window[:], table_blocks[k])
+            windows.append(window)
 
         edge_sums = psum.tile([P, EDGES], F32, name="edge_sums")
         for k in range(BLOCKS):
@@ -47,7 +45,7 @@ def tile_gather_matmul_kernel(tc, table, w, b, offs, out):
                 )
                 nc.tensor.matmul(
                     edge_sums[:],
-                    weights[t][:, k, :],
+                    weights[:, t, k, :],
                     picked,
                     start=(k == 0 and t == 0),
                     stop=(k == BLOCKS - 1 and t == ENDS - 1),

@@ -10,6 +10,7 @@ ENDS = 2
 EDGES = 256
 OUT_FEATURES = 128
 LIST_COLUMNS = EDGES // 16
+ROW_ALIGN = 256
 
 FLOPS = 2 * ENDS * FEATURES * OUT_FEATURES * EDGES
 
@@ -23,7 +24,9 @@ def tile_gather_matmul_kernel(tc, table, w, b, offs, out):
         offsets = held.tile([P, ENDS * LIST_COLUMNS], U16, name="offsets")
         nc.sync.dma_start(offsets[:], offs)
 
-        weights = held.tile([P, ENDS, BLOCKS, OUT_FEATURES], BF16, name="weights")
+        weights = held.tile(
+            [P, ENDS, BLOCKS, OUT_FEATURES], BF16, name="weights", align_bytes=ROW_ALIGN
+        )
         nc.scalar.dma_start(weights[:], w.rearrange("t (p k) m -> p t k m", k=BLOCKS))
 
         bias = held.tile([P, 1], F32, name="bias")
@@ -32,7 +35,7 @@ def tile_gather_matmul_kernel(tc, table, w, b, offs, out):
         table_blocks = table.rearrange("(p k) s -> k p s", k=BLOCKS)
         windows = []
         for k in range(BLOCKS):
-            window = held.tile([P, NODES], BF16, name="window%d" % k)
+            window = held.tile([P, NODES], BF16, name="window%d" % k, align_bytes=ROW_ALIGN)
             queue = nc.sync if k % 2 == 0 else nc.scalar
             queue.dma_start(window[:], table_blocks[k])
             windows.append(window)
@@ -51,7 +54,7 @@ def tile_gather_matmul_kernel(tc, table, w, b, offs, out):
                     stop=(k == BLOCKS - 1 and t == ENDS - 1),
                 )
 
-        result = held.tile([P, EDGES], F32, name="result")
+        result = held.tile([P, EDGES], F32, name="result", align_bytes=ROW_ALIGN)
         nc.vector.tensor_scalar(
             result[:], edge_sums[:], bias[:, 0:1], None, mybir.AluOpType.add
         )

@@ -29,9 +29,6 @@ def tile_gather_matmul_kernel(tc, table, w, b, offs, out):
         )
         nc.scalar.dma_start(weights[:], w.rearrange("t (p k) m -> p t k m", k=BLOCKS))
 
-        bias = held.tile([P, 1], F32, name="bias")
-        nc.gpsimd.dma_start(bias[:], b)
-
         table_blocks = table.rearrange("(p k) s -> k p s", k=BLOCKS)
         windows = []
         for k in range(BLOCKS):
@@ -39,6 +36,9 @@ def tile_gather_matmul_kernel(tc, table, w, b, offs, out):
             queue = nc.sync if k % 2 == 0 else nc.scalar
             queue.dma_start(window[:], table_blocks[k])
             windows.append(window)
+
+        bias = held.tile([P, 1], F32, name="bias")
+        nc.scalar.dma_start(bias[:], b)
 
         edge_sums = psum.tile([P, EDGES], F32, name="edge_sums")
         for k in range(BLOCKS):

@@ -27,18 +27,17 @@ def tile_gather_matmul_kernel(tc, table, w, b, offs, out):
         weights = held.tile(
             [P, ENDS, BLOCKS, OUT_FEATURES], BF16, name="weights", align_bytes=ROW_ALIGN
         )
-        nc.scalar.dma_start(weights[:], w.rearrange("t (p k) m -> p t k m", k=BLOCKS))
+        nc.sync.dma_start(weights[:], w.rearrange("t (p k) m -> p t k m", k=BLOCKS))
 
         table_blocks = table.rearrange("(p k) s -> k p s", k=BLOCKS)
         windows = []
         for k in range(BLOCKS):
             window = held.tile([P, NODES], BF16, name="window%d" % k, align_bytes=ROW_ALIGN)
-            queue = nc.sync if k % 2 == 0 else nc.scalar
-            queue.dma_start(window[:], table_blocks[k])
+            nc.sync.dma_start(window[:], table_blocks[k])
             windows.append(window)
 
         bias = held.tile([P, 1], F32, name="bias")
-        nc.scalar.dma_start(bias[:], b)
+        nc.sync.dma_start(bias[:], b)
 
         edge_sums = psum.tile([P, EDGES], F32, name="edge_sums")
         for k in range(BLOCKS):

@@ -21,20 +21,21 @@ def tile_gather_matmul_kernel(tc, table, w, b, offs, out):
         tc.tile_pool(name="held", bufs=1) as held,
         tc.psum_pool(name="psum", bufs=1) as psum,
     ):
-        offsets = held.tile([P, ENDS * LIST_COLUMNS], U16, name="offsets")
-        nc.sync.dma_start(offsets[:], offs)
-
         weights = held.tile(
             [P, ENDS, BLOCKS, OUT_FEATURES], BF16, name="weights", align_bytes=ROW_ALIGN
         )
-        nc.sync.dma_start(weights[:], w.rearrange("t (p k) m -> p t k m", k=BLOCKS))
+        windows = [
+            held.tile([P, NODES], BF16, name="window%d" % k, align_bytes=ROW_ALIGN)
+            for k in range(BLOCKS)
+        ]
+        offsets = held.tile([P, ENDS * LIST_COLUMNS], U16, name="offsets")
 
         table_blocks = table.rearrange("(p k) s -> k p s", k=BLOCKS)
-        windows = []
-        for k in range(BLOCKS):
-            window = held.tile([P, NODES], BF16, name="window%d" % k, align_bytes=ROW_ALIGN)
-            nc.sync.dma_start(window[:], table_blocks[k])
-            windows.append(window)
+        nc.sync.dma_start(windows[0][:], table_blocks[0])
+        nc.sync.dma_start(offsets[:], offs)
+        nc.sync.dma_start(weights[:], w.rearrange("t (p k) m -> p t k m", k=BLOCKS))
+        for k in range(1, BLOCKS):
+            nc.sync.dma_start(windows[k][:], table_blocks[k])
 
         bias = held.tile([P, 1], F32, name="bias")
         nc.sync.dma_start(bias[:], b)

import concourse.mybir as mybir

BF16, F32, U16 = mybir.dt.bfloat16, mybir.dt.float32, mybir.dt.uint16

P = 128
NODES = 1024
FEATURES = 512
BLOCKS = FEATURES // P
ENDS = 2
EDGES = 256
OUT_FEATURES = 128
LIST_COLUMNS = EDGES // 16
ROW_ALIGN = 256

FLOPS = 2 * ENDS * FEATURES * OUT_FEATURES * EDGES


def tile_gather_matmul_kernel(tc, table, w, b, offs, out):
    nc = tc.nc
    with (
        tc.tile_pool(name="held", bufs=1) as held,
        tc.psum_pool(name="psum", bufs=1) as psum,
    ):
        weights = held.tile(
            [P, ENDS, BLOCKS, OUT_FEATURES], BF16, name="weights", align_bytes=ROW_ALIGN
        )
        windows = [
            held.tile([P, NODES], BF16, name="window%d" % k, align_bytes=ROW_ALIGN)
            for k in range(BLOCKS)
        ]
        offsets = held.tile([P, ENDS * LIST_COLUMNS], U16, name="offsets")

        table_blocks = table.rearrange("(p k) s -> k p s", k=BLOCKS)
        nc.sync.dma_start(windows[0][:], table_blocks[0])
        nc.sync.dma_start(offsets[:], offs)
        nc.sync.dma_start(weights[:], w.rearrange("t (p k) m -> p t k m", k=BLOCKS))
        for k in range(1, BLOCKS):
            nc.sync.dma_start(windows[k][:], table_blocks[k])

        bias = held.tile([P, 1], F32, name="bias")
        nc.sync.dma_start(bias[:], b)

        edge_sums = psum.tile([P, EDGES], F32, name="edge_sums")
        for k in range(BLOCKS):
            for t in range(ENDS):
                picked = windows[k][:].indirect(
                    offsets[:, t * LIST_COLUMNS : (t + 1) * LIST_COLUMNS]
                )
                nc.tensor.matmul(
                    edge_sums[:],
                    weights[:, t, k, :],
                    picked,
                    start=(k == 0 and t == 0),
                    stop=(k == BLOCKS - 1 and t == ENDS - 1),
                )

        result = held.tile([P, EDGES], F32, name="result", align_bytes=ROW_ALIGN)
        nc.vector.tensor_scalar(
            result[:], edge_sums[:], bias[:, 0:1], None, mybir.AluOpType.add
        )
        nc.sync.dma_start(out, result[:])
